import numpy as np
import ml_dtypes


def mxq(x, axis, fmt="e4m3"):
    dtype, down = {"e4m3": (ml_dtypes.float8_e4m3fn, 7), "e5m2": (ml_dtypes.float8_e5m2, 14)}[fmt]
    v = np.moveaxis(np.asarray(x, np.float32).astype(ml_dtypes.bfloat16).astype(np.float64), axis, -1)
    blocks = v.reshape(v.shape[:-1] + (-1, 32))
    amax = np.abs(blocks).max(-1, keepdims=True)
    byte = np.maximum(np.where(amax > 0, np.frexp(amax)[1] - 1 + 127, 0) - down, 1)
    scale = np.exp2(byte - 127.0)
    codes = (blocks / scale).astype(np.float32).astype(dtype).astype(np.float64)
    return np.moveaxis((codes * scale).reshape(v.shape), -1, axis)


WIDE = False


def mx_kscale(k):
    if not WIDE:
        return np.ones(k)
    levels = np.array([30, -30])
    if k % 512:
        return np.exp2(np.random.permutation(np.resize(levels, k // 32))).repeat(32)
    a = np.empty((k // 512, 16))
    for p in range(k // 512):
        a[p, :8] = np.random.permutation(np.resize(levels, 8))
        for g in range(8):
            far = levels[np.abs(levels - a[p, g]) >= 10]
            a[p, g + 8] = far[np.random.randint(len(far))]
    return np.exp2(a.ravel()).repeat(32)


def f64(x):
    return np.asarray(x).astype(np.float64)


E2M1 = np.array([0.0, 0.5, 1.0, 1.5, 2.0, 3.0, 4.0, 6.0, -0.0, -0.5, -1.0, -1.5, -2.0, -3.0, -4.0, -6.0])


def pack_weight(w, fmt):
    k, n = w.shape
    w = f64(np.asarray(w, np.float32).astype(ml_dtypes.bfloat16)).reshape(k // 32, 32, n)
    amax = np.abs(w).max(1)
    if fmt == "e4m3":
        byte = np.frexp(amax)[1] - 1 + 127 - 7
    else:
        mant, ex = np.frexp(amax / 6.0)
        byte = np.where(mant > 0.5, ex, ex - 1) + 127
    byte = np.clip(np.where(amax > 0, byte, 1), 1, 254)
    scaled = (w * np.exp2(127.0 - byte)[:, None, :]).reshape(k, n).astype(np.float32)
    by_word = np.ascontiguousarray(scaled.reshape(k // 512, 128, 4, n).transpose(0, 1, 3, 2))
    if fmt == "e4m3":
        words = by_word.astype(ml_dtypes.float8_e4m3fn).view(np.uint8)
    else:
        c = by_word.astype(ml_dtypes.float4_e2m1fn).view(np.uint8) & 0xF
        words = (c[..., 0::2] | (c[..., 1::2] << 4)).reshape(k // 512, 128, 2 * n)
    return np.ascontiguousarray(words), np.ascontiguousarray(byte.astype(np.uint8).reshape(k // 512, 16, n))


def unpack_weight(words, scales, fmt):
    g, _, n = scales.shape
    words = np.ascontiguousarray(words).reshape(g, 128, n, -1)
    if fmt == "e4m3":
        vals = words.view(ml_dtypes.float8_e4m3fn).astype(np.float64)
    else:
        nib = np.empty((g, 128, n, 4), np.uint8)
        nib[..., 0::2] = words & 0xF
        nib[..., 1::2] = words >> 4
        vals = E2M1[nib]
    vals = vals * np.repeat(np.exp2(scales.astype(np.float64) - 127.0), 8, axis=1)[..., None]
    return vals.transpose(0, 1, 3, 2).reshape(g * 512, n)


K, T, N = 2048, 512, 512


def setup_inputs():
    n = np.random.standard_normal
    fk = mx_kscale(K)
    wap = pack_weight(n((K, N)) * 1 / np.sqrt(K) * fk[:, None], "e2m1")
    wbp = pack_weight(n((K, N)) * 1 / np.sqrt(K) * fk[:, None], "e4m3")
    return {
        "xf": (n((K, T))).astype(np.float32),
        "fa": (np.random.uniform(0.5, 2.0, (K, 1)) / fk[:, None]).astype(np.float32),
        "fb": (np.random.uniform(0.5, 2.0, (K, 1)) / fk[:, None]).astype(np.float32),
        "wa_words": wap[0],
        "wa_scales": wap[1],
        "wb_words": wbp[0],
        "wb_scales": wbp[1],
    }


def reference(xf, fa, fb, wa_words, wa_scales, wb_words, wb_scales):
    wau = unpack_weight(wa_words, wa_scales, "e2m1")
    wbu = unpack_weight(wb_words, wb_scales, "e4m3")
    s = f64(xf) * np.abs(f64(xf)) * f64(fa)
    v = f64(xf) * f64(fb)
    sq = mxq(s, 0, "e5m2")
    vq = mxq(v, 0, "e4m3")
    y = wau.T @ sq + wbu.T @ vq
    return y

@@ -1,0 +1,217 @@
+from contextlib import ExitStack
+
+import concourse.mybir as mybir
+
+K, T, N = 2048, 512, 512
+FLOPS = 2 * 2 * K * T * N
+
+F32 = mybir.dt.float32
+BF16 = mybir.dt.bfloat16
+I32 = mybir.dt.int32
+U32 = mybir.dt.uint32
+U8 = mybir.dt.uint8
+E4M3 = mybir.dt.float8_e4m3fn_x4
+E5M2 = mybir.dt.float8_e5m2_x4
+E2M1 = mybir.dt.float4_e2m1fn_x4
+ACT = mybir.ActivationFunctionType
+ALU = mybir.AluOpType
+
+P = 128
+PACK = 4
+PASSES = K // (P * PACK)
+N_TILES = N // P
+PAIR = 2
+FACTOR_PITCH = 8
+
+FIRST_PIECES = ((0, 128), (128, 128), (256, 256))
+HALVES = ((0, 256), (256, 256))
+WHOLE = ((0, 512),)
+LAST_PIECES = ((0, 256), (256, 128), (384, 128))
+
+
+def by_pairs(rows):
+    return rows.rearrange("p j (c i) -> p c j i", i=PAIR)
+
+
+def packed_by_pairs(grouped):
+    return grouped.rearrange("p (c i j) -> p c j i", i=PAIR, j=PACK)
+
+
+def tile_mix_signed_squares_and_values_kernel(tc, xf, fa, fb, wa_words, wa_scales, wb_words, wb_scales, out):
+    nc = tc.nc
+    last = PASSES - 1
+
+    with ExitStack() as ctx:
+        pool = ctx.enter_context(tc.tile_pool(name="sbuf", bufs=1))
+        psum = ctx.enter_context(tc.psum_pool(name="psum", bufs=1))
+        ctx.enter_context(tc.manual_schedule())
+
+        def sb(name, shape, dtype):
+            return pool.tile(shape, dtype, name=name, align_bytes=64)
+
+        wa_plane = sb("wa_plane", [P, PASSES, N], U8)
+        wb_plane = sb("wb_plane", [P, PASSES, N], U8)
+        nc.vector.memset(wb_plane[:].rearrange("p g n -> p (g n)").bitcast(I32), 0)
+        nc.vector.memset(wa_plane[:].rearrange("p g n -> p (g n)").bitcast(I32), 0)
+
+        fa_t = sb("fa_t", [P, PASSES, FACTOR_PITCH], F32)
+        fb_t = sb("fb_t", [P, PASSES, FACTOR_PITCH], F32)
+        nc.scalar.dma_start(out=fb_t[:, :, 0:PACK], in_=fb.rearrange("(g p j) o -> p g (j o)", p=P, j=PACK))
+        nc.scalar.dma_start(out=fa_t[:, :, 0:PACK], in_=fa.rearrange("(g p j) o -> p g (j o)", p=P, j=PACK))
+
+        x_rows = xf.rearrange("(g p j) t -> g p j t", p=P, j=PACK)
+        x_tiles = {}
+
+        def load_x(g, pieces):
+            for t0, w in pieces:
+                x_tiles[g, t0] = sb("x_%d_%d" % (g, t0), [P, PACK, w], F32)
+                nc.sync.dma_start(out=x_tiles[g, t0][:], in_=x_rows[g][:, :, t0 : t0 + w])
+
+        def x_piece(g, t0, w):
+            if (g, t0) in x_tiles and x_tiles[g, t0].shape[2] == w:
+                return x_tiles[g, t0][:]
+            return x_tiles[g, 0][:, :, t0 : t0 + w]
+
+        def load_scales(plane, scales):
+            for q in range(4):
+                nc.sync.dma_start(
+                    out=plane[32 * q : 32 * q + 4, :, :].bitcast(I32),
+                    in_=scales[:, 4 * q : 4 * q + 4, :].rearrange("g r n -> r g n").bitcast(I32),
+                )
+
+        load_x(0, FIRST_PIECES)
+        load_x(1, WHOLE)
+        load_x(2, WHOLE)
+        load_scales(wb_plane, wb_scales)
+        load_scales(wa_plane, wa_scales)
+        wb_t = sb("wb_t", [P, PASSES, PACK * N], U8)
+        nc.sync.dma_start(out=wb_t[:].bitcast(I32), in_=wb_words.rearrange("g p n r -> p g (n r)").bitcast(I32))
+        load_x(3, WHOLE)
+        wa_t = sb("wa_t", [P, PASSES, 2 * N], U8)
+        nc.sync.dma_start(out=wa_t[:].bitcast(I32), in_=wa_words.rearrange("g p b -> p g b").bitcast(I32))
+
+        xa, xabs, xb = {}, {}, {}
+
+        def scale_rows(dst, g, t0, w, factors):
+            for j in range(PACK):
+                nc.scalar.activation(out=dst[:, j, :], in_=x_piece(g, t0, w)[:, j, :], func=ACT.Copy, scale=factors[:, g, j : j + 1])
+
+        def prepare_s(g, t0, w):
+            xabs[g, t0] = sb("xabs_%d_%d" % (g, t0), [P, PACK, w], F32)
+            xa[g, t0] = sb("xa_%d_%d" % (g, t0), [P, PACK, w], F32)
+            nc.scalar.activation(out=xabs[g, t0][:], in_=x_piece(g, t0, w), func=ACT.Abs)
+            scale_rows(xa[g, t0], g, t0, w, fa_t)
+
+        def prepare_v(g, t0, w):
+            xb[g, t0] = sb("xb_%d_%d" % (g, t0), [P, PACK, w], F32)
+            scale_rows(xb[g, t0], g, t0, w, fb_t)
+
+        s_pieces = [FIRST_PIECES, WHOLE, WHOLE, HALVES]
+        for g in range(PASSES):
+            for t0, w in s_pieces[g]:
+                prepare_s(g, t0, w)
+        for t0, w in LAST_PIECES:
+            prepare_v(last, t0, w)
+
+        s_bf = [sb("s_bf_%d" % g, [P, PACK * T], BF16) for g in range(PASSES)]
+        v_bf = [sb("v_bf_%d" % g, [P, PACK * T], BF16) for g in range(PASSES)]
+        s_codes = [sb("s_codes_%d" % g, [P, T], U32) for g in range(PASSES)]
+        v_codes = [sb("v_codes_%d" % g, [P, T], U32) for g in range(PASSES)]
+        s_plane = [sb("s_plane_%d" % g, [P, T], U8) for g in range(PASSES)]
+        v_plane = [sb("v_plane_%d" % g, [P, T], U8) for g in range(PASSES)]
+
+        def make_s(g, t0, w):
+            nc.vector.tensor_tensor(
+                out=packed_by_pairs(s_bf[g][:, PACK * t0 : PACK * (t0 + w)]),
+                in0=by_pairs(xa[g, t0][:]),
+                in1=by_pairs(xabs[g, t0][:]),
+                op=ALU.mult,
+            )
+
+        def make_v(g, t0, w):
+            factors = fb_t[:, g, 0:PACK].unsqueeze(1).unsqueeze(3).to_broadcast([P, w // PAIR, PACK, PAIR])
+            nc.vector.tensor_tensor(
+                out=packed_by_pairs(v_bf[g][:, PACK * t0 : PACK * (t0 + w)]),
+                in0=by_pairs(x_piece(g, t0, w)),
+                in1=factors,
+                op=ALU.mult,
+            )
+
+        def pack_v(g, t0, w):
+            nc.vector.tensor_copy(out=packed_by_pairs(v_bf[g][:, PACK * t0 : PACK * (t0 + w)]), in_=by_pairs(xb[g, t0][:]))
+
+        def quantize(bf, codes, plane, fmt, t0, w):
+            nc.vector.quantize_mx(out=codes[:, t0 : t0 + w].bitcast(fmt), scales=plane[:, t0 : t0 + w], in_=bf[:, PACK * t0 : PACK * (t0 + w)])
+
+        def quantize_s(g, t0=0, w=T):
+            quantize(s_bf[g], s_codes[g], s_plane[g], E5M2, t0, w)
+
+        def quantize_v(g, t0=0, w=T):
+            quantize(v_bf[g], v_codes[g], v_plane[g], E4M3, t0, w)
+
+        for t0, w in FIRST_PIECES:
+            make_v(0, t0, w)
+        make_s(0, 0, 128)
+        make_s(0, 128, 128)
+        quantize_v(0)
+        make_v(1, 0, T)
+        make_s(0, 256, 256)
+        quantize_v(1)
+        make_v(2, 0, T)
+        quantize_s(0)
+        make_s(1, 0, T)
+        quantize_v(2)
+        make_s(2, 0, T)
+        quantize_s(1)
+        make_s(3, 0, 256)
+        quantize_s(2)
+        make_s(3, 256, 256)
+        quantize_s(3, 0, 256)
+        quantize_s(3, 256, 256)
+        pack_v(3, 0, 256)
+        pack_v(3, 256, 128)
+        quantize_v(3, 0, 256)
+        pack_v(3, 384, 128)
+        quantize_v(3, 256, 128)
+        quantize_v(3, 384, 128)
+
+        acc = [psum.tile([P, T], F32, name="acc_%d" % m) for m in range(N_TILES)]
+
+        def multiply_s(g):
+            for m in range(N_TILES):
+                nc.tensor.matmul_mx(
+                    out=acc[m][:],
+                    lhsT=wa_t[:, g, 2 * P * m : 2 * P * (m + 1)].bitcast(E2M1),
+                    lhsT_scale=wa_plane[:, g, P * m : P * (m + 1)],
+                    rhs=s_codes[g][:].bitcast(E5M2),
+                    rhs_scale=s_plane[g][:],
+                    start=False,
+                    stop=False,
+                )
+
+        def multiply_v(g, t0, w):
+            for m in range(N_TILES):
+                nc.tensor.matmul_mx(
+                    out=acc[m][:, t0 : t0 + w],
+                    lhsT=wb_t[:, g, PACK * P * m : PACK * P * (m + 1)].bitcast(E4M3),
+                    lhsT_scale=wb_plane[:, g, P * m : P * (m + 1)],
+                    rhs=v_codes[g][:, t0 : t0 + w].bitcast(E4M3),
+                    rhs_scale=v_plane[g][:, t0 : t0 + w],
+                    start=(g == 0),
+                    stop=(g == last and t0 + w == T),
+                )
+
+        for g in range(last):
+            multiply_v(g, 0, T)
+        for g in range(PASSES):
+            multiply_s(g)
+        for t0, w in LAST_PIECES:
+            multiply_v(last, t0, w)
+
+        for m in range(N_TILES):
+            result = sb("result_%d" % m, [P, T], F32)
+            if m % 2 == 0:
+                nc.scalar.copy(out=result[:], in_=acc[m][:])
+            else:
+                nc.vector.tensor_copy(out=result[:], in_=acc[m][:])
+            nc.sync.dma_start(out=out[P * m : P * (m + 1), :], in_=result[:])

@@ -26,7 +26,8 @@ FACTOR_PITCH = 8
 FIRST_PIECES = ((0, 128), (128, 128), (256, 256))
 HALVES = ((0, 256), (256, 256))
 WHOLE = ((0, 512),)
-LAST_PIECES = ((0, 256), (256, 128), (384, 128))
+EARLY = 384
+LATE = T - EARLY
 
 
 def by_pairs(rows):
@@ -50,14 +51,16 @@ def tile_mix_signed_squares_and_values_kernel(tc, xf, fa, fb, wa_words, wa_scale
             return pool.tile(shape, dtype, name=name, align_bytes=64)
 
         wa_plane = sb("wa_plane", [P, PASSES, N], U8)
-        wb_plane = sb("wb_plane", [P, PASSES, N], U8)
-        nc.vector.memset(wb_plane[:].rearrange("p g n -> p (g n)").bitcast(I32), 0)
+        wb_plane = sb("wb_plane", [P, N], U8)
+        nc.vector.memset(wb_plane[:].bitcast(I32), 0)
         nc.vector.memset(wa_plane[:].rearrange("p g n -> p (g n)").bitcast(I32), 0)
 
         fa_t = sb("fa_t", [P, PASSES, FACTOR_PITCH], F32)
         fb_t = sb("fb_t", [P, PASSES, FACTOR_PITCH], F32)
-        nc.scalar.dma_start(out=fb_t[:, :, 0:PACK], in_=fb.rearrange("(g p j) o -> p g (j o)", p=P, j=PACK))
-        nc.scalar.dma_start(out=fa_t[:, :, 0:PACK], in_=fa.rearrange("(g p j) o -> p g (j o)", p=P, j=PACK))
+        fa_rows = fa.rearrange("(g p j) o -> p g (j o)", p=P, j=PACK)
+        fb_rows = fb.rearrange("(g p j) o -> p g (j o)", p=P, j=PACK)
+        nc.scalar.dma_start(out=fb_t[:, 0, 0:PACK], in_=fb_rows[:, 0, :])
+        nc.scalar.dma_start(out=fa_t[:, 0, 0:PACK], in_=fa_rows[:, 0, :])
 
         x_rows = xf.rearrange("(g p j) t -> g p j t", p=P, j=PACK)
         x_tiles = {}
@@ -68,9 +71,8 @@ def tile_mix_signed_squares_and_values_kernel(tc, xf, fa, fb, wa_words, wa_scale
                 nc.sync.dma_start(out=x_tiles[g, t0][:], in_=x_rows[g][:, :, t0 : t0 + w])
 
         def x_piece(g, t0, w):
-            if (g, t0) in x_tiles and x_tiles[g, t0].shape[2] == w:
-                return x_tiles[g, t0][:]
-            return x_tiles[g, 0][:, :, t0 : t0 + w]
+            start = max(t for gg, t in x_tiles if gg == g and t <= t0)
+            return x_tiles[g, start][:, :, t0 - start : t0 - start + w]
 
         def load_scales(plane, scales):
             for q in range(4):
@@ -80,15 +82,18 @@ def tile_mix_signed_squares_and_values_kernel(tc, xf, fa, fb, wa_words, wa_scale
                 )
 
         load_x(0, FIRST_PIECES)
-        load_x(1, WHOLE)
+        nc.sync.dma_start(out=fb_t[:, 1:PASSES, 0:PACK], in_=fb_rows[:, 1:PASSES, :])
+        nc.sync.dma_start(out=fa_t[:, 1:PASSES, 0:PACK], in_=fa_rows[:, 1:PASSES, :])
+        load_x(1, HALVES)
         load_x(2, WHOLE)
-        load_scales(wb_plane, wb_scales)
         load_scales(wa_plane, wa_scales)
-        wb_t = sb("wb_t", [P, PASSES, PACK * N], U8)
-        nc.sync.dma_start(out=wb_t[:].bitcast(I32), in_=wb_words.rearrange("g p n r -> p g (n r)").bitcast(I32))
-        load_x(3, WHOLE)
+        for q in range(4):
+            nc.sync.dma_start(out=wb_plane[32 * q : 32 * q + 16, :].bitcast(I32), in_=wb_scales[:, 4 * q : 4 * q + 4, :].bitcast(I32))
         wa_t = sb("wa_t", [P, PASSES, 2 * N], U8)
         nc.sync.dma_start(out=wa_t[:].bitcast(I32), in_=wa_words.rearrange("g p b -> p g b").bitcast(I32))
+        load_x(3, WHOLE)
+        wb_t = sb("wb_t", [P, PASSES, PACK * N], U8)
+        nc.sync.dma_start(out=wb_t[:].bitcast(I32), in_=wb_words.rearrange("g p n r -> p g (n r)").bitcast(I32))
 
         xa, xabs, xb = {}, {}, {}
 
@@ -106,12 +111,12 @@ def tile_mix_signed_squares_and_values_kernel(tc, xf, fa, fb, wa_words, wa_scale
             xb[g, t0] = sb("xb_%d_%d" % (g, t0), [P, PACK, w], F32)
             scale_rows(xb[g, t0], g, t0, w, fb_t)
 
-        s_pieces = [FIRST_PIECES, WHOLE, WHOLE, HALVES]
+        s_pieces = [FIRST_PIECES, HALVES, WHOLE, HALVES]
         for g in range(PASSES):
             for t0, w in s_pieces[g]:
                 prepare_s(g, t0, w)
-        for t0, w in LAST_PIECES:
-            prepare_v(last, t0, w)
+        for g in range(PASSES):
+            prepare_v(g, EARLY, LATE)
 
         s_bf = [sb("s_bf_%d" % g, [P, PACK * T], BF16) for g in range(PASSES)]
         v_bf = [sb("v_bf_%d" % g, [P, PACK * T], BF16) for g in range(PASSES)]
@@ -149,33 +154,42 @@ def tile_mix_signed_squares_and_values_kernel(tc, xf, fa, fb, wa_words, wa_scale
         def quantize_v(g, t0=0, w=T):
             quantize(v_bf[g], v_codes[g], v_plane[g], E4M3, t0, w)
 
-        for t0, w in FIRST_PIECES:
-            make_v(0, t0, w)
+        def quantize_v_early(g):
+            quantize_v(g, 0, 256)
+            quantize_v(g, 256, 128)
+
+        make_v(0, 0, 128)
+        make_v(0, 128, 128)
         make_s(0, 0, 128)
+        make_v(0, 256, 128)
         make_s(0, 128, 128)
-        quantize_v(0)
-        make_v(1, 0, T)
+        quantize_v_early(0)
+        make_v(1, 0, 256)
+        make_v(1, 256, 128)
         make_s(0, 256, 256)
-        quantize_v(1)
-        make_v(2, 0, T)
+        quantize_v_early(1)
         quantize_s(0)
-        make_s(1, 0, T)
-        quantize_v(2)
-        make_s(2, 0, T)
+        make_s(1, 0, 256)
+        make_v(2, 0, EARLY)
+        make_s(1, 256, 256)
+        quantize_v_early(2)
         quantize_s(1)
-        make_s(3, 0, 256)
+        make_v(3, 0, EARLY)
+        make_s(2, 0, T)
+        quantize_v_early(3)
         quantize_s(2)
+        make_s(3, 0, 256)
         make_s(3, 256, 256)
         quantize_s(3, 0, 256)
         quantize_s(3, 256, 256)
-        pack_v(3, 0, 256)
-        pack_v(3, 256, 128)
-        quantize_v(3, 0, 256)
-        pack_v(3, 384, 128)
-        quantize_v(3, 256, 128)
-        quantize_v(3, 384, 128)
+        pack_v(0, EARLY, LATE)
+        for g in range(1, PASSES):
+            pack_v(g, EARLY, LATE)
+            quantize_v(g - 1, EARLY, LATE)
+        quantize_v(last, EARLY, LATE)
 
         acc = [psum.tile([P, T], F32, name="acc_%d" % m) for m in range(N_TILES)]
+        acc_late = [psum.tile([P, LATE], F32, name="acc_late_%d" % m) for m in range(N_TILES)]
 
         def multiply_s(g):
             for m in range(N_TILES):
@@ -185,33 +199,44 @@ def tile_mix_signed_squares_and_values_kernel(tc, xf, fa, fb, wa_words, wa_scale
                     lhsT_scale=wa_plane[:, g, P * m : P * (m + 1)],
                     rhs=s_codes[g][:].bitcast(E5M2),
                     rhs_scale=s_plane[g][:],
-                    start=False,
-                    stop=False,
+                    start=(g == 0),
+                    stop=(g == last),
                 )
 
-        def multiply_v(g, t0, w):
+        def multiply_v(dst, g, t0, w, start=False, stop=False):
             for m in range(N_TILES):
                 nc.tensor.matmul_mx(
-                    out=acc[m][:, t0 : t0 + w],
+                    out=dst[m],
                     lhsT=wb_t[:, g, PACK * P * m : PACK * P * (m + 1)].bitcast(E4M3),
-                    lhsT_scale=wb_plane[:, g, P * m : P * (m + 1)],
+                    lhsT_scale=wb_plane[4 * g :, P * m : P * (m + 1)],
                     rhs=v_codes[g][:, t0 : t0 + w].bitcast(E4M3),
                     rhs_scale=v_plane[g][:, t0 : t0 + w],
-                    start=(g == 0),
-                    stop=(g == last and t0 + w == T),
+                    start=start,
+                    stop=stop,
                 )
 
-        for g in range(last):
-            multiply_v(g, 0, T)
-        for g in range(PASSES):
-            multiply_s(g)
-        for t0, w in LAST_PIECES:
-            multiply_v(last, t0, w)
+        def multiply_v_early(g):
+            for t0, w in ((0, 256), (256, 128)):
+                multiply_v([bank[:, t0 : t0 + w] for bank in acc], g, t0, w)
 
+        multiply_s(0)
+        multiply_s(1)
+        for g in range(PASSES):
+            multiply_v_early(g)
+        multiply_s(2)
+        multiply_s(3)
+        for g in range(PASSES):
+            multiply_v([bank[:] for bank in acc_late], g, EARLY, LATE, start=(g == 0), stop=(g == last))
+
+        result = [sb("result_%d" % m, [P, T], F32) for m in range(N_TILES)]
         for m in range(N_TILES):
-            result = sb("result_%d" % m, [P, T], F32)
-            if m % 2 == 0:
-                nc.scalar.copy(out=result[:], in_=acc[m][:])
+            if m < N_TILES - 1:
+                nc.scalar.copy(out=result[m][:], in_=acc[m][:])
             else:
-                nc.vector.tensor_copy(out=result[:], in_=acc[m][:])
-            nc.sync.dma_start(out=out[P * m : P * (m + 1), :], in_=result[:])
+                nc.vector.tensor_copy(out=result[m][:], in_=acc[m][:])
+        for m in (0, 1, 3, 2):
+            nc.sync.dma_start(out=out[P * m : P * (m + 1), 0:EARLY], in_=result[m][:, 0:EARLY])
+        for m in (0, 1, 3, 2):
+            late = sb("late_%d" % m, [P, LATE], F32)
+            nc.vector.tensor_tensor(out=late[:], in0=acc_late[m][:], in1=result[m][:, EARLY:T], op=ALU.add)
+            nc.sync.dma_start(out=out[P * m : P * (m + 1), EARLY:T], in_=late[:])

@@ -70,30 +70,44 @@ def tile_mix_signed_squares_and_values_kernel(tc, xf, fa, fb, wa_words, wa_scale
                 x_tiles[g, t0] = sb("x_%d_%d" % (g, t0), [P, PACK, w], F32)
                 nc.sync.dma_start(out=x_tiles[g, t0][:], in_=x_rows[g][:, :, t0 : t0 + w])
 
-        def x_piece(g, t0, w):
-            start = max(t for gg, t in x_tiles if gg == g and t <= t0)
-            return x_tiles[g, start][:, :, t0 - start : t0 - start + w]
+        def piece(tiles, g, t0, w):
+            start = max(t for gg, t in tiles if gg == g and t <= t0)
+            return tiles[g, start][:, :, t0 - start : t0 - start + w]
 
-        def load_scales(plane, scales):
-            for q in range(4):
-                nc.sync.dma_start(
-                    out=plane[32 * q : 32 * q + 4, :, :].bitcast(I32),
-                    in_=scales[:, 4 * q : 4 * q + 4, :].rearrange("g r n -> r g n").bitcast(I32),
-                )
+        def x_piece(g, t0, w):
+            return piece(x_tiles, g, t0, w)
+
+        def load_wa_scales(q):
+            nc.sync.dma_start(
+                out=wa_plane[32 * q : 32 * q + 4, :, :].bitcast(I32),
+                in_=wa_scales[:, 4 * q : 4 * q + 4, :].rearrange("g r n -> r g n").bitcast(I32),
+            )
+
+        def load_wb_scales(q):
+            nc.sync.dma_start(out=wb_plane[32 * q : 32 * q + 16, :].bitcast(I32), in_=wb_scales[:, 4 * q : 4 * q + 4, :].bitcast(I32))
+
+        wa_t = sb("wa_t", [P, PASSES, 2 * N], U8)
+        wb_t = [sb("wb_t_%d" % h, [P, 2, PACK * N], U8) for h in range(2)]
+        wb_rows = wb_words.rearrange("g p n r -> p g (n r)")
 
         load_x(0, FIRST_PIECES)
         nc.sync.dma_start(out=fb_t[:, 1:PASSES, 0:PACK], in_=fb_rows[:, 1:PASSES, :])
         nc.sync.dma_start(out=fa_t[:, 1:PASSES, 0:PACK], in_=fa_rows[:, 1:PASSES, :])
-        load_x(1, HALVES)
+        load_x(1, HALVES[:1])
+        load_wa_scales(0)
+        load_wa_scales(1)
+        load_x(1, HALVES[1:])
+        load_wa_scales(2)
+        load_wa_scales(3)
         load_x(2, WHOLE)
-        load_scales(wa_plane, wa_scales)
-        for q in range(4):
-            nc.sync.dma_start(out=wb_plane[32 * q : 32 * q + 16, :].bitcast(I32), in_=wb_scales[:, 4 * q : 4 * q + 4, :].bitcast(I32))
-        wa_t = sb("wa_t", [P, PASSES, 2 * N], U8)
+        load_wb_scales(0)
+        load_wb_scales(1)
         nc.sync.dma_start(out=wa_t[:].bitcast(I32), in_=wa_words.rearrange("g p b -> p g b").bitcast(I32))
+        load_wb_scales(2)
+        load_wb_scales(3)
+        nc.sync.dma_start(out=wb_t[0][:].bitcast(I32), in_=wb_rows[:, 0:2, :].bitcast(I32))
         load_x(3, WHOLE)
-        wb_t = sb("wb_t", [P, PASSES, PACK * N], U8)
-        nc.sync.dma_start(out=wb_t[:].bitcast(I32), in_=wb_words.rearrange("g p n r -> p g (n r)").bitcast(I32))
+        nc.sync.dma_start(out=wb_t[1][:].bitcast(I32), in_=wb_rows[:, 2:4, :].bitcast(I32))
 
         xa, xabs, xb = {}, {}, {}
 
@@ -128,8 +142,8 @@ def tile_mix_signed_squares_and_values_kernel(tc, xf, fa, fb, wa_words, wa_scale
         def make_s(g, t0, w):
             nc.vector.tensor_tensor(
                 out=packed_by_pairs(s_bf[g][:, PACK * t0 : PACK * (t0 + w)]),
-                in0=by_pairs(xa[g, t0][:]),
-                in1=by_pairs(xabs[g, t0][:]),
+                in0=by_pairs(piece(xa, g, t0, w)),
+                in1=by_pairs(piece(xabs, g, t0, w)),
                 op=ALU.mult,
             )
 
@@ -173,15 +187,14 @@ def tile_mix_signed_squares_and_values_kernel(tc, xf, fa, fb, wa_words, wa_scale
         make_v(2, 0, EARLY)
         make_s(1, 256, 256)
         quantize_v_early(2)
-        quantize_s(1)
         make_v(3, 0, EARLY)
-        make_s(2, 0, T)
+        quantize_s(1)
         quantize_v_early(3)
-        quantize_s(2)
-        make_s(3, 0, 256)
-        make_s(3, 256, 256)
-        quantize_s(3, 0, 256)
-        quantize_s(3, 256, 256)
+        for g in (2, 3):
+            for t0, w in HALVES:
+                make_s(g, t0, w)
+            for t0, w in HALVES:
+                quantize_s(g, t0, w)
         pack_v(0, EARLY, LATE)
         for g in range(1, PASSES):
             pack_v(g, EARLY, LATE)
@@ -207,7 +220,7 @@ def tile_mix_signed_squares_and_values_kernel(tc, xf, fa, fb, wa_words, wa_scale
             for m in range(N_TILES):
                 nc.tensor.matmul_mx(
                     out=dst[m],
-                    lhsT=wb_t[:, g, PACK * P * m : PACK * P * (m + 1)].bitcast(E4M3),
+                    lhsT=wb_t[g // 2][:, g % 2, PACK * P * m : PACK * P * (m + 1)].bitcast(E4M3),
                     lhsT_scale=wb_plane[4 * g :, P * m : P * (m + 1)],
                     rhs=v_codes[g][:, t0 : t0 + w].bitcast(E4M3),
                     rhs_scale=v_plane[g][:, t0 : t0 + w],
@@ -220,10 +233,12 @@ def tile_mix_signed_squares_and_values_kernel(tc, xf, fa, fb, wa_words, wa_scale
                 multiply_v([bank[:, t0 : t0 + w] for bank in acc], g, t0, w)
 
         multiply_s(0)
+        multiply_v_early(1)
+        multiply_v_early(2)
         multiply_s(1)
-        for g in range(PASSES):
-            multiply_v_early(g)
+        multiply_v_early(3)
         multiply_s(2)
+        multiply_v_early(0)
         multiply_s(3)
         for g in range(PASSES):
             multiply_v([bank[:] for bank in acc_late], g, EARLY, LATE, start=(g == 0), stop=(g == last))

@@ -1,6 +1,7 @@
 from contextlib import ExitStack
 
 import concourse.mybir as mybir
+from concourse.masks import make_identity
 
 K, T, N = 2048, 512, 512
 FLOPS = 2 * 2 * K * T * N
@@ -18,10 +19,10 @@ ALU = mybir.AluOpType
 
 P = 128
 PACK = 4
-PASSES = K // (P * PACK)
+K_PASS = P * PACK
+PASSES = K // K_PASS
 N_TILES = N // P
 PAIR = 2
-FACTOR_PITCH = 8
 
 FIRST_PIECES = ((0, 128), (128, 128), (256, 256))
 HALVES = ((0, 256), (256, 256))
@@ -55,12 +56,14 @@ def tile_mix_signed_squares_and_values_kernel(tc, xf, fa, fb, wa_words, wa_scale
         nc.vector.memset(wb_plane[:].bitcast(I32), 0)
         nc.vector.memset(wa_plane[:].rearrange("p g n -> p (g n)").bitcast(I32), 0)
 
-        fa_t = sb("fa_t", [P, PASSES, FACTOR_PITCH], F32)
-        fb_t = sb("fb_t", [P, PASSES, FACTOR_PITCH], F32)
-        fa_rows = fa.rearrange("(g p j) o -> p g (j o)", p=P, j=PACK)
-        fb_rows = fb.rearrange("(g p j) o -> p g (j o)", p=P, j=PACK)
-        nc.scalar.dma_start(out=fb_t[:, 0, 0:PACK], in_=fb_rows[:, 0, :])
-        nc.scalar.dma_start(out=fa_t[:, 0, 0:PACK], in_=fa_rows[:, 0, :])
+        fa_first = sb("fa_first", [P, PACK], F32)
+        fb_first = sb("fb_first", [P, PACK], F32)
+        nc.scalar.dma_start(out=fb_first[:], in_=fb[0:K_PASS, :].rearrange("(p j) o -> p (j o)", j=PACK))
+        nc.scalar.dma_start(out=fa_first[:], in_=fa[0:K_PASS, :].rearrange("(p j) o -> p (j o)", j=PACK))
+        factor_rows = sb("factor_rows", [P, K_PASS], F32)
+        nc.gpsimd.memset(factor_rows[:], 0.0)
+        identity = sb("identity", [P, P], F32)
+        make_identity(nc, identity[:])
 
         x_rows = xf.rearrange("(g p j) t -> g p j t", p=P, j=PACK)
         x_tiles = {}
@@ -91,29 +94,31 @@ def tile_mix_signed_squares_and_values_kernel(tc, xf, fa, fb, wa_words, wa_scale
         wb_rows = wb_words.rearrange("g p n r -> p g (n r)")
 
         load_x(0, FIRST_PIECES)
-        nc.sync.dma_start(out=fb_t[:, 1:PASSES, 0:PACK], in_=fb_rows[:, 1:PASSES, :])
-        nc.sync.dma_start(out=fa_t[:, 1:PASSES, 0:PACK], in_=fa_rows[:, 1:PASSES, :])
-        load_x(1, HALVES[:1])
-        load_wa_scales(0)
-        load_wa_scales(1)
-        load_x(1, HALVES[1:])
-        load_wa_scales(2)
-        load_wa_scales(3)
+        nc.sync.dma_start(out=factor_rows[0:last, :], in_=fb[K_PASS:K, :].rearrange("(g k) o -> g (k o)", g=last))
+        nc.sync.dma_start(out=factor_rows[last : 2 * last, :], in_=fa[K_PASS:K, :].rearrange("(g k) o -> g (k o)", g=last))
+        load_x(1, HALVES)
         load_x(2, WHOLE)
-        load_wb_scales(0)
-        load_wb_scales(1)
+        for q in range(4):
+            load_wa_scales(q)
         nc.sync.dma_start(out=wa_t[:].bitcast(I32), in_=wa_words.rearrange("g p b -> p g b").bitcast(I32))
-        load_wb_scales(2)
-        load_wb_scales(3)
-        nc.sync.dma_start(out=wb_t[0][:].bitcast(I32), in_=wb_rows[:, 0:2, :].bitcast(I32))
         load_x(3, WHOLE)
+        for q in range(4):
+            load_wb_scales(q)
+        nc.sync.dma_start(out=wb_t[0][:].bitcast(I32), in_=wb_rows[:, 0:2, :].bitcast(I32))
         nc.sync.dma_start(out=wb_t[1][:].bitcast(I32), in_=wb_rows[:, 2:4, :].bitcast(I32))
+
+        turned = psum.tile([P, PACK, P], F32, name="turned", tag="late_0")
+        for j in range(PACK):
+            nc.tensor.transpose(turned[:, j, :], factor_rows[:, j:K_PASS:PACK], identity[:])
+        factors = sb("factors", [P, 2 * last, PACK], F32)
+        fb_t = [fb_first[:]] + [factors[:, g, :] for g in range(last)]
+        fa_t = [fa_first[:]] + [factors[:, last + g, :] for g in range(last)]
 
         xa, xabs, xb = {}, {}, {}
 
-        def scale_rows(dst, g, t0, w, factors):
+        def scale_rows(dst, g, t0, w, table):
             for j in range(PACK):
-                nc.scalar.activation(out=dst[:, j, :], in_=x_piece(g, t0, w)[:, j, :], func=ACT.Copy, scale=factors[:, g, j : j + 1])
+                nc.scalar.activation(out=dst[:, j, :], in_=x_piece(g, t0, w)[:, j, :], func=ACT.Copy, scale=table[g][:, j : j + 1])
 
         def prepare_s(g, t0, w):
             xabs[g, t0] = sb("xabs_%d_%d" % (g, t0), [P, PACK, w], F32)
@@ -124,13 +129,6 @@ def tile_mix_signed_squares_and_values_kernel(tc, xf, fa, fb, wa_words, wa_scale
         def prepare_v(g, t0, w):
             xb[g, t0] = sb("xb_%d_%d" % (g, t0), [P, PACK, w], F32)
             scale_rows(xb[g, t0], g, t0, w, fb_t)
-
-        s_pieces = [FIRST_PIECES, HALVES, WHOLE, HALVES]
-        for g in range(PASSES):
-            for t0, w in s_pieces[g]:
-                prepare_s(g, t0, w)
-        for g in range(PASSES):
-            prepare_v(g, EARLY, LATE)
 
         s_bf = [sb("s_bf_%d" % g, [P, PACK * T], BF16) for g in range(PASSES)]
         v_bf = [sb("v_bf_%d" % g, [P, PACK * T], BF16) for g in range(PASSES)]
@@ -148,11 +146,11 @@ def tile_mix_signed_squares_and_values_kernel(tc, xf, fa, fb, wa_words, wa_scale
             )
 
         def make_v(g, t0, w):
-            factors = fb_t[:, g, 0:PACK].unsqueeze(1).unsqueeze(3).to_broadcast([P, w // PAIR, PACK, PAIR])
+            spread = fb_t[g].unsqueeze(1).unsqueeze(3).to_broadcast([P, w // PAIR, PACK, PAIR])
             nc.vector.tensor_tensor(
                 out=packed_by_pairs(v_bf[g][:, PACK * t0 : PACK * (t0 + w)]),
                 in0=by_pairs(x_piece(g, t0, w)),
-                in1=factors,
+                in1=spread,
                 op=ALU.mult,
             )
 
@@ -172,12 +170,20 @@ def tile_mix_signed_squares_and_values_kernel(tc, xf, fa, fb, wa_words, wa_scale
             quantize_v(g, 0, 256)
             quantize_v(g, 256, 128)
 
+        for t0, w in FIRST_PIECES:
+            prepare_s(0, t0, w)
         make_v(0, 0, 128)
         make_v(0, 128, 128)
         make_s(0, 0, 128)
         make_v(0, 256, 128)
         make_s(0, 128, 128)
+        nc.vector.tensor_copy(out=factors[:], in_=turned[:, :, 0 : 2 * last].rearrange("p j r -> p r j"))
         quantize_v_early(0)
+        for g, pieces in ((1, HALVES), (2, WHOLE), (3, HALVES)):
+            for t0, w in pieces:
+                prepare_s(g, t0, w)
+        for g in range(PASSES):
+            prepare_v(g, EARLY, LATE)
         make_v(1, 0, 256)
         make_v(1, 256, 128)
         make_s(0, 256, 256)
@@ -202,7 +208,7 @@ def tile_mix_signed_squares_and_values_kernel(tc, xf, fa, fb, wa_words, wa_scale
         quantize_v(last, EARLY, LATE)
 
         acc = [psum.tile([P, T], F32, name="acc_%d" % m) for m in range(N_TILES)]
-        acc_late = [psum.tile([P, LATE], F32, name="acc_late_%d" % m) for m in range(N_TILES)]
+        acc_late = [psum.tile([P, LATE], F32, name="acc_late_%d" % m, tag="late_%d" % m) for m in range(N_TILES)]
 
         def multiply_s(g):
             for m in range(N_TILES):

from contextlib import ExitStack

import concourse.mybir as mybir
from concourse.masks import make_identity

K, T, N = 2048, 512, 512
FLOPS = 2 * 2 * K * T * N

F32 = mybir.dt.float32
BF16 = mybir.dt.bfloat16
I32 = mybir.dt.int32
U32 = mybir.dt.uint32
U8 = mybir.dt.uint8
E4M3 = mybir.dt.float8_e4m3fn_x4
E5M2 = mybir.dt.float8_e5m2_x4
E2M1 = mybir.dt.float4_e2m1fn_x4
ACT = mybir.ActivationFunctionType
ALU = mybir.AluOpType

P = 128
PACK = 4
K_PASS = P * PACK
PASSES = K // K_PASS
N_TILES = N // P
PAIR = 2

FIRST_PIECES = ((0, 128), (128, 128), (256, 256))
HALVES = ((0, 256), (256, 256))
WHOLE = ((0, 512),)
EARLY = 384
LATE = T - EARLY


def by_pairs(rows):
    return rows.rearrange("p j (c i) -> p c j i", i=PAIR)


def packed_by_pairs(grouped):
    return grouped.rearrange("p (c i j) -> p c j i", i=PAIR, j=PACK)


def tile_mix_signed_squares_and_values_kernel(tc, xf, fa, fb, wa_words, wa_scales, wb_words, wb_scales, out):
    nc = tc.nc
    last = PASSES - 1

    with ExitStack() as ctx:
        pool = ctx.enter_context(tc.tile_pool(name="sbuf", bufs=1))
        psum = ctx.enter_context(tc.psum_pool(name="psum", bufs=1))
        ctx.enter_context(tc.manual_schedule())

        def sb(name, shape, dtype):
            return pool.tile(shape, dtype, name=name, align_bytes=64)

        wa_plane = sb("wa_plane", [P, PASSES, N], U8)
        wb_plane = sb("wb_plane", [P, N], U8)
        nc.vector.memset(wb_plane[:].bitcast(I32), 0)
        nc.vector.memset(wa_plane[:].rearrange("p g n -> p (g n)").bitcast(I32), 0)

        fa_first = sb("fa_first", [P, PACK], F32)
        fb_first = sb("fb_first", [P, PACK], F32)
        nc.scalar.dma_start(out=fb_first[:], in_=fb[0:K_PASS, :].rearrange("(p j) o -> p (j o)", j=PACK))
        nc.scalar.dma_start(out=fa_first[:], in_=fa[0:K_PASS, :].rearrange("(p j) o -> p (j o)", j=PACK))
        factor_rows = sb("factor_rows", [P, K_PASS], F32)
        nc.gpsimd.memset(factor_rows[:], 0.0)
        identity = sb("identity", [P, P], F32)
        make_identity(nc, identity[:])

        x_rows = xf.rearrange("(g p j) t -> g p j t", p=P, j=PACK)
        x_tiles = {}

        def load_x(g, pieces):
            for t0, w in pieces:
                x_tiles[g, t0] = sb("x_%d_%d" % (g, t0), [P, PACK, w], F32)
                nc.sync.dma_start(out=x_tiles[g, t0][:], in_=x_rows[g][:, :, t0 : t0 + w])

        def piece(tiles, g, t0, w):
            start = max(t for gg, t in tiles if gg == g and t <= t0)
            return tiles[g, start][:, :, t0 - start : t0 - start + w]

        def x_piece(g, t0, w):
            return piece(x_tiles, g, t0, w)

        def load_wa_scales(q):
            nc.sync.dma_start(
                out=wa_plane[32 * q : 32 * q + 4, :, :].bitcast(I32),
                in_=wa_scales[:, 4 * q : 4 * q + 4, :].rearrange("g r n -> r g n").bitcast(I32),
            )

        def load_wb_scales(q):
            nc.sync.dma_start(out=wb_plane[32 * q : 32 * q + 16, :].bitcast(I32), in_=wb_scales[:, 4 * q : 4 * q + 4, :].bitcast(I32))

        wa_t = sb("wa_t", [P, PASSES, 2 * N], U8)
        wb_t = [sb("wb_t_%d" % h, [P, 2, PACK * N], U8) for h in range(2)]
        wb_rows = wb_words.rearrange("g p n r -> p g (n r)")

        load_x(0, FIRST_PIECES)
        nc.sync.dma_start(out=factor_rows[0:last, :], in_=fb[K_PASS:K, :].rearrange("(g k) o -> g (k o)", g=last))
        nc.sync.dma_start(out=factor_rows[last : 2 * last, :], in_=fa[K_PASS:K, :].rearrange("(g k) o -> g (k o)", g=last))
        load_x(1, HALVES)
        load_x(2, WHOLE)
        for q in range(4):
            load_wa_scales(q)
        nc.sync.dma_start(out=wa_t[:].bitcast(I32), in_=wa_words.rearrange("g p b -> p g b").bitcast(I32))
        load_x(3, WHOLE)
        for q in range(4):
            load_wb_scales(q)
        nc.sync.dma_start(out=wb_t[0][:].bitcast(I32), in_=wb_rows[:, 0:2, :].bitcast(I32))
        nc.sync.dma_start(out=wb_t[1][:].bitcast(I32), in_=wb_rows[:, 2:4, :].bitcast(I32))

        turned = psum.tile([P, PACK, P], F32, name="turned", tag="late_0")
        for j in range(PACK):
            nc.tensor.transpose(turned[:, j, :], factor_rows[:, j:K_PASS:PACK], identity[:])
        factors = sb("factors", [P, 2 * last, PACK], F32)
        fb_t = [fb_first[:]] + [factors[:, g, :] for g in range(last)]
        fa_t = [fa_first[:]] + [factors[:, last + g, :] for g in range(last)]

        xa, xabs, xb = {}, {}, {}

        def scale_rows(dst, g, t0, w, table):
            for j in range(PACK):
                nc.scalar.activation(out=dst[:, j, :], in_=x_piece(g, t0, w)[:, j, :], func=ACT.Copy, scale=table[g][:, j : j + 1])

        def prepare_s(g, t0, w):
            xabs[g, t0] = sb("xabs_%d_%d" % (g, t0), [P, PACK, w], F32)
            xa[g, t0] = sb("xa_%d_%d" % (g, t0), [P, PACK, w], F32)
            nc.scalar.activation(out=xabs[g, t0][:], in_=x_piece(g, t0, w), func=ACT.Abs)
            scale_rows(xa[g, t0], g, t0, w, fa_t)

        def prepare_v(g, t0, w):
            xb[g, t0] = sb("xb_%d_%d" % (g, t0), [P, PACK, w], F32)
            scale_rows(xb[g, t0], g, t0, w, fb_t)

        s_bf = [sb("s_bf_%d" % g, [P, PACK * T], BF16) for g in range(PASSES)]
        v_bf = [sb("v_bf_%d" % g, [P, PACK * T], BF16) for g in range(PASSES)]
        s_codes = [sb("s_codes_%d" % g, [P, T], U32) for g in range(PASSES)]
        v_codes = [sb("v_codes_%d" % g, [P, T], U32) for g in range(PASSES)]
        s_plane = [sb("s_plane_%d" % g, [P, T], U8) for g in range(PASSES)]
        v_plane = [sb("v_plane_%d" % g, [P, T], U8) for g in range(PASSES)]

        def make_s(g, t0, w):
            nc.vector.tensor_tensor(
                out=packed_by_pairs(s_bf[g][:, PACK * t0 : PACK * (t0 + w)]),
                in0=by_pairs(piece(xa, g, t0, w)),
                in1=by_pairs(piece(xabs, g, t0, w)),
                op=ALU.mult,
            )

        def make_v(g, t0, w):
            spread = fb_t[g].unsqueeze(1).unsqueeze(3).to_broadcast([P, w // PAIR, PACK, PAIR])
            nc.vector.tensor_tensor(
                out=packed_by_pairs(v_bf[g][:, PACK * t0 : PACK * (t0 + w)]),
                in0=by_pairs(x_piece(g, t0, w)),
                in1=spread,
                op=ALU.mult,
            )

        def pack_v(g, t0, w):
            nc.vector.tensor_copy(out=packed_by_pairs(v_bf[g][:, PACK * t0 : PACK * (t0 + w)]), in_=by_pairs(xb[g, t0][:]))

        def quantize(bf, codes, plane, fmt, t0, w):
            nc.vector.quantize_mx(out=codes[:, t0 : t0 + w].bitcast(fmt), scales=plane[:, t0 : t0 + w], in_=bf[:, PACK * t0 : PACK * (t0 + w)])

        def quantize_s(g, t0=0, w=T):
            quantize(s_bf[g], s_codes[g], s_plane[g], E5M2, t0, w)

        def quantize_v(g, t0=0, w=T):
            quantize(v_bf[g], v_codes[g], v_plane[g], E4M3, t0, w)

        def quantize_v_early(g):
            quantize_v(g, 0, 256)
            quantize_v(g, 256, 128)

        for t0, w in FIRST_PIECES:
            prepare_s(0, t0, w)
        make_v(0, 0, 128)
        make_v(0, 128, 128)
        make_s(0, 0, 128)
        make_v(0, 256, 128)
        make_s(0, 128, 128)
        nc.vector.tensor_copy(out=factors[:], in_=turned[:, :, 0 : 2 * last].rearrange("p j r -> p r j"))
        quantize_v_early(0)
        for g, pieces in ((1, HALVES), (2, WHOLE), (3, HALVES)):
            for t0, w in pieces:
                prepare_s(g, t0, w)
        for g in range(PASSES):
            prepare_v(g, EARLY, LATE)
        make_v(1, 0, 256)
        make_v(1, 256, 128)
        make_s(0, 256, 256)
        quantize_v_early(1)
        quantize_s(0)
        make_s(1, 0, 256)
        make_v(2, 0, EARLY)
        make_s(1, 256, 256)
        quantize_v_early(2)
        make_v(3, 0, EARLY)
        quantize_s(1)
        quantize_v_early(3)
        for g in (2, 3):
            for t0, w in HALVES:
                make_s(g, t0, w)
            for t0, w in HALVES:
                quantize_s(g, t0, w)
        pack_v(0, EARLY, LATE)
        for g in range(1, PASSES):
            pack_v(g, EARLY, LATE)
            quantize_v(g - 1, EARLY, LATE)
        quantize_v(last, EARLY, LATE)

        acc = [psum.tile([P, T], F32, name="acc_%d" % m) for m in range(N_TILES)]
        acc_late = [psum.tile([P, LATE], F32, name="acc_late_%d" % m, tag="late_%d" % m) for m in range(N_TILES)]

        def multiply_s(g):
            for m in range(N_TILES):
                nc.tensor.matmul_mx(
                    out=acc[m][:],
                    lhsT=wa_t[:, g, 2 * P * m : 2 * P * (m + 1)].bitcast(E2M1),
                    lhsT_scale=wa_plane[:, g, P * m : P * (m + 1)],
                    rhs=s_codes[g][:].bitcast(E5M2),
                    rhs_scale=s_plane[g][:],
                    start=(g == 0),
                    stop=(g == last),
                )

        def multiply_v(dst, g, t0, w, start=False, stop=False):
            for m in range(N_TILES):
                nc.tensor.matmul_mx(
                    out=dst[m],
                    lhsT=wb_t[g // 2][:, g % 2, PACK * P * m : PACK * P * (m + 1)].bitcast(E4M3),
                    lhsT_scale=wb_plane[4 * g :, P * m : P * (m + 1)],
                    rhs=v_codes[g][:, t0 : t0 + w].bitcast(E4M3),
                    rhs_scale=v_plane[g][:, t0 : t0 + w],
                    start=start,
                    stop=stop,
                )

        def multiply_v_early(g):
            for t0, w in ((0, 256), (256, 128)):
                multiply_v([bank[:, t0 : t0 + w] for bank in acc], g, t0, w)

        multiply_s(0)
        multiply_v_early(1)
        multiply_v_early(2)
        multiply_s(1)
        multiply_v_early(3)
        multiply_s(2)
        multiply_v_early(0)
        multiply_s(3)
        for g in range(PASSES):
            multiply_v([bank[:] for bank in acc_late], g, EARLY, LATE, start=(g == 0), stop=(g == last))

        result = [sb("result_%d" % m, [P, T], F32) for m in range(N_TILES)]
        for m in range(N_TILES):
            if m < N_TILES - 1:
                nc.scalar.copy(out=result[m][:], in_=acc[m][:])
            else:
                nc.vector.tensor_copy(out=result[m][:], in_=acc[m][:])
        for m in (0, 1, 3, 2):
            nc.sync.dma_start(out=out[P * m : P * (m + 1), 0:EARLY], in_=result[m][:, 0:EARLY])
        for m in (0, 1, 3, 2):
            late = sb("late_%d" % m, [P, LATE], F32)
            nc.vector.tensor_tensor(out=late[:], in0=acc_late[m][:], in1=result[m][:, EARLY:T], op=ALU.add)
            nc.sync.dma_start(out=out[P * m : P * (m + 1), EARLY:T], in_=late[:])
